import numpy as np, ml_dtypes
CORES = [113,118,241,246]
N = 4
import mx_ref
NC, G = 512, 4
C = np.float32(0.047)
BF = ml_dtypes.bfloat16
def cut(t, i, w=512):
    return t[:, w * i:w * i + w]
def tile(rs):
    return np.stack(rs, axis=2).reshape(128, -1).astype(BF)
def act(Z):
    return [np.maximum(z, 0) * C for z in Z]
def setup_inputs(rng):
    def f(*shape):
        return mx_ref.flush((rng.standard_normal(shape, dtype=np.float32) * np.exp2(rng.integers(-2, 3, shape[:-1] + (1,)))).astype(BF))
    return {"x": f(N, 128, 4 * NC), "res": f(N, 128, 4 * NC), "w1": f(N, 128, 512), "w2": f(N, 128, 2 * 512)}
def setup_inputs_blocks(rng):
    d = setup_inputs(rng)
    for k in ("x", "w1", "w2", "res"): d[k] = mx_ref.spread(d[k], rng, 4)
    return d
def setup_inputs_wide(rng):
    d = setup_inputs(rng)
    for k in ("x", "w1", "w2", "res"): d[k] = mx_ref.flush((d[k].astype(np.float32) * np.exp2(rng.integers(-6, 7, (N, 1, 1))).astype(np.float32)).astype(BF))
    return d
def reference(x, res, w1, w2):
    W = [mx_ref.quantize(w1[j]) for j in range(N)]; H = []
    for r in range(N):
        X = mx_ref.quantize(x[r]); e = res[r].astype(np.float32)
        R = act([mx_ref.matmul(W[(r + i) % N], X) for i in range(G)])
        H.append(mx_ref.quantize(tile([R[b] + e[:, b::4] for b in range(4)])))
    y = np.zeros((N, 128, NC), np.float32)
    for r in range(N):
        y[r] = mx_ref.matmul(mx_ref.quantize(cut(w2[r], 0)), H[r]) + mx_ref.matmul(mx_ref.quantize(cut(w2[r], 1)), H[(r + 1) % N])
    return {"y": y}

@@ -1,0 +1,177 @@
+from concourse.bass import DstId, RemoteDMATransfer
+from concourse.mybir import dt, AluOpType, ActivationFunctionType
+
+N = 4
+NC = 512
+WC = 128
+HALF = NC // 2
+SCALE = 0.047
+NUNITS = 1 + 2 * (N - 1)
+
+SCRATCH = {
+    "w1t": ("sbuf", [128, 4 * WC], "bfloat16"),
+    "xt": ("sbuf", [128, 4 * NC], "bfloat16"),
+    "et": ("sbuf", [128, 4 * NC], "bfloat16"),
+    "w2t": ("sbuf", [128, 8 * WC], "bfloat16"),
+    "w1q": ("sbuf", [128, N * WC], "float8_e4m3fn_x4"),
+    "w1s": ("sbuf", [128, N * WC], "uint8"),
+    "xq": ("sbuf", [128, NC], "float8_e4m3fn_x4"),
+    "xs": ("sbuf", [128, NC], "uint8"),
+    "w2q": ("sbuf", [128, 2 * WC], "float8_e4m3fn_x4"),
+    "w2s": ("sbuf", [128, 2 * WC], "uint8"),
+    "at": ("sbuf", [128, 4 * NC], "float32"),
+    "ht": ("sbuf", [128, 4 * NC], "bfloat16"),
+    "hq": ("sbuf", [128, NC], "float8_e4m3fn_x4"),
+    "hs": ("sbuf", [128, NC], "uint8"),
+    "gq": ("sbuf", [128, NC], "float8_e4m3fn_x4"),
+    "gs": ("sbuf", [128, NC], "uint8"),
+    "yt": ("sbuf", [128, NC], "float32"),
+    "ps": ("psum", [128, 8 * 512], "float32"),
+}
+SEMAPHORES = (["ld_w1", "ld_x", "ld_e", "ld_w2", "q_w1", "q_x", "q_w2", "q_h", "ah", "sent", "y0", "y1", "c0", "c1", "st"]
+              + ["aw%d" % j for j in range(N)]
+              + ["%s%d" % (k, u) for k in "zad" for u in range(NUNITS)])
+
+
+def _count(mask):
+    return bin(mask).count("1")
+
+
+def _same_chip(topo, a, b):
+    return topo.host(a) == topo.host(b) and topo.chip(a) == topo.chip(b)
+
+
+def _w1_rounds(topo, cores, q):
+    me = cores[q]
+    others = [(q + i) % N for i in range(1, N)]
+    off = [p for p in others if not _same_chip(topo, me, cores[p])]
+    leave = 0
+    for p in off:
+        leave |= topo.mask(me, cores[p])
+    first = [p for p in off if not _same_chip(topo, cores[p], cores[(p - 1) % N])]
+    rounds = [[(p, topo.mask(me, cores[p]))] for p in first]
+    later = []
+    for p in others:
+        if p in first:
+            continue
+        m = topo.mask(me, cores[p])
+        if p not in off and (m & ~leave):
+            m &= ~leave
+        for rnd in later:
+            if all((m & m2) == 0 for _, m2 in rnd):
+                rnd.append((p, m))
+                break
+        else:
+            later.append([(p, m)])
+    return rounds + later
+
+
+def rank_program(g, core, T, topo):
+    r = T.rank_of(core)
+    if r is None:
+        return
+    cores = list(T.cores)
+    S = T.sem
+    u8 = dt.uint8
+
+    def slot(j):
+        return slice(j * WC, (j + 1) * WC)
+
+    def arrival(q):
+        for k, rnd in enumerate(_w1_rounds(topo, cores, q)):
+            for p, m in rnd:
+                if p == r:
+                    return k, not _same_chip(topo, cores[q], core), _count(m)
+    srcs = sorted([(r + i) % N for i in range(1, N)], key=lambda q: arrival(q)[:2])
+
+    units = [(r, 0, NC, 0)]
+    for k, j in enumerate(srcs):
+        for h in range(2):
+            units.append((j, h * HALF, HALF, 1 + 2 * k + h))
+    ybank = (0, 7)
+
+    g.sync.dma_start(T.w1t[:], T.w1[:]).then_inc(S.ld_w1, 16)
+    g.scalar.dma_start(T.xt[:], T.x[:]).then_inc(S.ld_x, 16)
+    g.sync.dma_start(T.et[:], T.res[:]).then_inc(S.ld_e, 16)
+    g.sync.wait_ge(S.z1, 1)
+    g.sync.dma_start(T.w2t[:], T.w2[:]).then_inc(S.ld_w2, 16)
+
+    sent = 0
+    g.wait_ge(S.q_w1, 1)
+    for rnd in _w1_rounds(topo, cores, r):
+        for buf, cast in ((T.w1q, True), (T.w1s, False)):
+            view = buf[:, slot(r)].bitcast(u8) if cast else buf[:, slot(r)]
+            trs = []
+            for p, m in rnd:
+                rid, pid = topo.addr(cores[p], core)
+                trs.append(RemoteDMATransfer(dst_ids=[DstId(rid=rid, pnc=pid)], dma_engine_mask=m,
+                                             remote_sem=S["aw%d" % r], src=view, dst=view))
+                sent += _count(m)
+            g.remote_dma_fused(trs, local_sem=S.sent)
+    hdst = cores[(r - 1) % N]
+    hmask = topo.mask(core, hdst)
+    rid, pid = topo.addr(hdst, core)
+    g.wait_ge(S.q_h, 1)
+    g.remote_dma(out_ap=T.gq[:].bitcast(u8), in_ap=T.hq[:].bitcast(u8), remote_sem=S.ah, local_sem=S.sent,
+                 pid=pid, routing_id=rid, dma_engine_mask=hmask)
+    g.remote_dma(out_ap=T.gs[:], in_ap=T.hs[:], remote_sem=S.ah, local_sem=S.sent,
+                 pid=pid, routing_id=rid, dma_engine_mask=hmask)
+    sent += 2 * _count(hmask)
+    g.wait_ge(S.sent, sent)
+
+    te = g.tensor
+    te.wait_ge(S.q_w1, 1)
+    te.wait_ge(S.q_x, 1)
+    seen = {r}
+    for u, (j, c0, n, bank) in enumerate(units):
+        if j not in seen:
+            te.wait_ge(S["aw%d" % j], 2 * arrival(j)[2])
+            seen.add(j)
+        te.matmul_mx(T.ps[:, bank * 512:bank * 512 + n], T.w1q[:, slot(j)], T.w1s[:, slot(j)],
+                     T.xq[:, c0:c0 + n], T.xs[:, c0:c0 + n], True, True).then_inc(S["z%d" % u], 1)
+    te.wait_ge(S.q_h, 1)
+    te.wait_ge(S.q_w2, 1)
+    for h in range(2):
+        o = T.ps[:, ybank[h] * 512:ybank[h] * 512 + HALF]
+        te.matmul_mx(o, T.w2q[:, slot(0)], T.w2s[:, slot(0)],
+                     T.hq[:, h * HALF:(h + 1) * HALF], T.hs[:, h * HALF:(h + 1) * HALF], True, False)
+    hsrc = cores[(r + 1) % N]
+    te.wait_ge(S.ah, 2 * _count(topo.mask(hsrc, core)))
+    for h in range(2):
+        o = T.ps[:, ybank[h] * 512:ybank[h] * 512 + HALF]
+        te.matmul_mx(o, T.w2q[:, slot(1)], T.w2s[:, slot(1)],
+                     T.gq[:, h * HALF:(h + 1) * HALF], T.gs[:, h * HALF:(h + 1) * HALF], False, True).then_inc(S["y%d" % h], 1)
+
+    sc = g.scalar
+    for u, (j, c0, n, bank) in enumerate(units):
+        b = (j - r) % N
+        sc.wait_ge(S["z%d" % u], 1)
+        sc.activation(T.at[:, b * NC + c0:b * NC + c0 + n], T.ps[:, bank * 512:bank * 512 + n],
+                      ActivationFunctionType.Relu, scale=SCALE).then_inc(S["a%d" % u], 1)
+    sc.wait_ge(S.y1, 1)
+    sc.activation(T.yt[:, HALF:NC], T.ps[:, ybank[1] * 512:ybank[1] * 512 + HALF],
+                  ActivationFunctionType.Copy).then_inc(S.c1, 1)
+
+    ve = g.vector
+    ve.wait_ge(S.ld_w1, 16)
+    ve.quantize_mx(T.w1q[:, slot(r)], T.w1s[:, slot(r)], T.w1t[:]).then_inc(S.q_w1, 1)
+    ve.wait_ge(S.ld_x, 16)
+    ve.quantize_mx(T.xq[:], T.xs[:], T.xt[:]).then_inc(S.q_x, 1)
+    ve.wait_ge(S.ld_e, 16)
+    for u, (j, c0, n, bank) in enumerate(units):
+        b = (j - r) % N
+        ve.wait_ge(S["a%d" % u], 1)
+        ve.tensor_tensor(T.ht[:, 4 * c0 + b:4 * (c0 + n):4], T.at[:, b * NC + c0:b * NC + c0 + n],
+                         T.et[:, 4 * c0 + b:4 * (c0 + n):4], AluOpType.add).then_inc(S["d%d" % u], 1)
+    for u in range(len(units)):
+        ve.wait_ge(S["d%d" % u], 1)
+    ve.quantize_mx(T.hq[:], T.hs[:], T.ht[:]).then_inc(S.q_h, 1)
+    ve.wait_ge(S.ld_w2, 16)
+    ve.quantize_mx(T.w2q[:], T.w2s[:], T.w2t[:]).then_inc(S.q_w2, 1)
+    ve.wait_ge(S.y0, 1)
+    ve.tensor_copy(T.yt[:, 0:HALF], T.ps[:, ybank[0] * 512:ybank[0] * 512 + HALF]).then_inc(S.c0, 1)
+
+    g.sync.wait_ge(S.c0, 1)
+    g.sync.wait_ge(S.c1, 1)
+    g.sync.dma_start(T.y[:], T.yt[:]).then_inc(S.st, 16)
+    g.sync.wait_ge(S.st, 16)

@@ -28,7 +28,8 @@ SCRATCH = {
     "yt": ("sbuf", [128, NC], "float32"),
     "ps": ("psum", [128, 8 * 512], "float32"),
 }
-SEMAPHORES = (["ld_w1", "ld_x", "ld_e", "ld_w2", "q_w1", "q_x", "q_w2", "q_h", "ah", "sent", "y0", "y1", "c0", "c1", "st"]
+SEMAPHORES = (["ld_w1", "ld_x", "ld_e", "ld_w2", "q_w1", "q_x", "q_w2", "q_h0", "q_h1", "ah0", "ah1", "sent",
+               "y0", "y1", "c0", "c1", "st"]
               + ["aw%d" % j for j in range(N)]
               + ["%s%d" % (k, u) for k in "zad" for u in range(NUNITS)])
 
@@ -77,6 +78,9 @@ def rank_program(g, core, T, topo):
     def slot(j):
         return slice(j * WC, (j + 1) * WC)
 
+    def half(h):
+        return slice(h * HALF, (h + 1) * HALF)
+
     def arrival(q):
         for k, rnd in enumerate(_w1_rounds(topo, cores, q)):
             for p, m in rnd:
@@ -85,8 +89,8 @@ def rank_program(g, core, T, topo):
     srcs = sorted([(r + i) % N for i in range(1, N)], key=lambda q: arrival(q)[:2])
 
     units = [(r, 0, NC, 0)]
-    for k, j in enumerate(srcs):
-        for h in range(2):
+    for h in range(2):
+        for k, j in enumerate(srcs):
             units.append((j, h * HALF, HALF, 1 + 2 * k + h))
     ybank = (0, 7)
 
@@ -111,12 +115,13 @@ def rank_program(g, core, T, topo):
     hdst = cores[(r - 1) % N]
     hmask = topo.mask(core, hdst)
     rid, pid = topo.addr(hdst, core)
-    g.wait_ge(S.q_h, 1)
-    g.remote_dma(out_ap=T.gq[:].bitcast(u8), in_ap=T.hq[:].bitcast(u8), remote_sem=S.ah, local_sem=S.sent,
-                 pid=pid, routing_id=rid, dma_engine_mask=hmask)
-    g.remote_dma(out_ap=T.gs[:], in_ap=T.hs[:], remote_sem=S.ah, local_sem=S.sent,
-                 pid=pid, routing_id=rid, dma_engine_mask=hmask)
-    sent += 2 * _count(hmask)
+    for h in range(2):
+        g.wait_ge(S["q_h%d" % h], 1)
+        g.remote_dma(out_ap=T.gq[:, half(h)].bitcast(u8), in_ap=T.hq[:, half(h)].bitcast(u8), remote_sem=S["ah%d" % h],
+                     local_sem=S.sent, pid=pid, routing_id=rid, dma_engine_mask=hmask)
+        g.remote_dma(out_ap=T.gs[:, half(h)], in_ap=T.hs[:, half(h)], remote_sem=S["ah%d" % h],
+                     local_sem=S.sent, pid=pid, routing_id=rid, dma_engine_mask=hmask)
+        sent += 2 * _count(hmask)
     g.wait_ge(S.sent, sent)
 
     te = g.tensor
@@ -129,18 +134,18 @@ def rank_program(g, core, T, topo):
             seen.add(j)
         te.matmul_mx(T.ps[:, bank * 512:bank * 512 + n], T.w1q[:, slot(j)], T.w1s[:, slot(j)],
                      T.xq[:, c0:c0 + n], T.xs[:, c0:c0 + n], True, True).then_inc(S["z%d" % u], 1)
-    te.wait_ge(S.q_h, 1)
+    te.wait_ge(S.q_h0, 1)
+    te.wait_ge(S.q_h1, 1)
     te.wait_ge(S.q_w2, 1)
     for h in range(2):
         o = T.ps[:, ybank[h] * 512:ybank[h] * 512 + HALF]
-        te.matmul_mx(o, T.w2q[:, slot(0)], T.w2s[:, slot(0)],
-                     T.hq[:, h * HALF:(h + 1) * HALF], T.hs[:, h * HALF:(h + 1) * HALF], True, False)
+        te.matmul_mx(o, T.w2q[:, slot(0)], T.w2s[:, slot(0)], T.hq[:, half(h)], T.hs[:, half(h)], True, False)
     hsrc = cores[(r + 1) % N]
-    te.wait_ge(S.ah, 2 * _count(topo.mask(hsrc, core)))
     for h in range(2):
+        te.wait_ge(S["ah%d" % h], 2 * _count(topo.mask(hsrc, core)))
         o = T.ps[:, ybank[h] * 512:ybank[h] * 512 + HALF]
-        te.matmul_mx(o, T.w2q[:, slot(1)], T.w2s[:, slot(1)],
-                     T.gq[:, h * HALF:(h + 1) * HALF], T.gs[:, h * HALF:(h + 1) * HALF], False, True).then_inc(S["y%d" % h], 1)
+        te.matmul_mx(o, T.w2q[:, slot(1)], T.w2s[:, slot(1)], T.gq[:, half(h)], T.gs[:, half(h)],
+                     False, True).then_inc(S["y%d" % h], 1)
 
     sc = g.scalar
     for u, (j, c0, n, bank) in enumerate(units):
@@ -149,7 +154,7 @@ def rank_program(g, core, T, topo):
         sc.activation(T.at[:, b * NC + c0:b * NC + c0 + n], T.ps[:, bank * 512:bank * 512 + n],
                       ActivationFunctionType.Relu, scale=SCALE).then_inc(S["a%d" % u], 1)
     sc.wait_ge(S.y1, 1)
-    sc.activation(T.yt[:, HALF:NC], T.ps[:, ybank[1] * 512:ybank[1] * 512 + HALF],
+    sc.activation(T.yt[:, half(1)], T.ps[:, ybank[1] * 512:ybank[1] * 512 + HALF],
                   ActivationFunctionType.Copy).then_inc(S.c1, 1)
 
     ve = g.vector
@@ -163,15 +168,18 @@ def rank_program(g, core, T, topo):
         ve.wait_ge(S["a%d" % u], 1)
         ve.tensor_tensor(T.ht[:, 4 * c0 + b:4 * (c0 + n):4], T.at[:, b * NC + c0:b * NC + c0 + n],
                          T.et[:, 4 * c0 + b:4 * (c0 + n):4], AluOpType.add).then_inc(S["d%d" % u], 1)
-    for u in range(len(units)):
-        ve.wait_ge(S["d%d" % u], 1)
-    ve.quantize_mx(T.hq[:], T.hs[:], T.ht[:]).then_inc(S.q_h, 1)
+        if u in (N - 1, 2 * N - 2):
+            h = 0 if u == N - 1 else 1
+            for v in range(0 if h == 0 else N, u + 1):
+                ve.wait_ge(S["d%d" % v], 1)
+            ve.quantize_mx(T.hq[:, half(h)], T.hs[:, half(h)],
+                           T.ht[:, 4 * h * HALF:4 * (h + 1) * HALF]).then_inc(S["q_h%d" % h], 1)
     ve.wait_ge(S.ld_w2, 16)
     ve.quantize_mx(T.w2q[:], T.w2s[:], T.w2t[:]).then_inc(S.q_w2, 1)
     ve.wait_ge(S.y0, 1)
-    ve.tensor_copy(T.yt[:, 0:HALF], T.ps[:, ybank[0] * 512:ybank[0] * 512 + HALF]).then_inc(S.c0, 1)
+    ve.tensor_copy(T.yt[:, half(0)], T.ps[:, ybank[0] * 512:ybank[0] * 512 + HALF]).then_inc(S.c0, 1)
 
-    g.sync.wait_ge(S.c0, 1)
-    g.sync.wait_ge(S.c1, 1)
-    g.sync.dma_start(T.y[:], T.yt[:]).then_inc(S.st, 16)
-    g.sync.wait_ge(S.st, 16)
+    for h in range(2):
+        g.sync.wait_ge(S["c%d" % h], 1)
+        g.sync.dma_start(T.y[:, half(h)], T.yt[:, half(h)]).then_inc(S.st, 16)
+    g.sync.wait_ge(S.st, 32)

from concourse.bass import DstId, RemoteDMATransfer
from concourse.mybir import dt, AluOpType, ActivationFunctionType

N = 4
NC = 512
WC = 128
HALF = NC // 2
SCALE = 0.047
NUNITS = 1 + 2 * (N - 1)

SCRATCH = {
    "w1t": ("sbuf", [128, 4 * WC], "bfloat16"),
    "xt": ("sbuf", [128, 4 * NC], "bfloat16"),
    "et": ("sbuf", [128, 4 * NC], "bfloat16"),
    "w2t": ("sbuf", [128, 8 * WC], "bfloat16"),
    "w1q": ("sbuf", [128, N * WC], "float8_e4m3fn_x4"),
    "w1s": ("sbuf", [128, N * WC], "uint8"),
    "xq": ("sbuf", [128, NC], "float8_e4m3fn_x4"),
    "xs": ("sbuf", [128, NC], "uint8"),
    "w2q": ("sbuf", [128, 2 * WC], "float8_e4m3fn_x4"),
    "w2s": ("sbuf", [128, 2 * WC], "uint8"),
    "at": ("sbuf", [128, 4 * NC], "float32"),
    "ht": ("sbuf", [128, 4 * NC], "bfloat16"),
    "hq": ("sbuf", [128, NC], "float8_e4m3fn_x4"),
    "hs": ("sbuf", [128, NC], "uint8"),
    "gq": ("sbuf", [128, NC], "float8_e4m3fn_x4"),
    "gs": ("sbuf", [128, NC], "uint8"),
    "yt": ("sbuf", [128, NC], "float32"),
    "ps": ("psum", [128, 8 * 512], "float32"),
}
SEMAPHORES = (["ld_w1", "ld_x", "ld_e", "ld_w2", "q_w1", "q_x", "q_w2", "q_h0", "q_h1", "ah0", "ah1", "sent",
               "y0", "y1", "c0", "c1", "st"]
              + ["aw%d" % j for j in range(N)]
              + ["%s%d" % (k, u) for k in "zad" for u in range(NUNITS)])


def _count(mask):
    return bin(mask).count("1")


def _same_chip(topo, a, b):
    return topo.host(a) == topo.host(b) and topo.chip(a) == topo.chip(b)


def _w1_rounds(topo, cores, q):
    me = cores[q]
    others = [(q + i) % N for i in range(1, N)]
    off = [p for p in others if not _same_chip(topo, me, cores[p])]
    leave = 0
    for p in off:
        leave |= topo.mask(me, cores[p])
    first = [p for p in off if not _same_chip(topo, cores[p], cores[(p - 1) % N])]
    rounds = [[(p, topo.mask(me, cores[p]))] for p in first]
    later = []
    for p in others:
        if p in first:
            continue
        m = topo.mask(me, cores[p])
        if p not in off and (m & ~leave):
            m &= ~leave
        for rnd in later:
            if all((m & m2) == 0 for _, m2 in rnd):
                rnd.append((p, m))
                break
        else:
            later.append([(p, m)])
    return rounds + later


def rank_program(g, core, T, topo):
    r = T.rank_of(core)
    if r is None:
        return
    cores = list(T.cores)
    S = T.sem
    u8 = dt.uint8

    def slot(j):
        return slice(j * WC, (j + 1) * WC)

    def half(h):
        return slice(h * HALF, (h + 1) * HALF)

    def arrival(q):
        for k, rnd in enumerate(_w1_rounds(topo, cores, q)):
            for p, m in rnd:
                if p == r:
                    return k, not _same_chip(topo, cores[q], core), _count(m)
    srcs = sorted([(r + i) % N for i in range(1, N)], key=lambda q: arrival(q)[:2])

    units = [(r, 0, NC, 0)]
    for h in range(2):
        for k, j in enumerate(srcs):
            units.append((j, h * HALF, HALF, 1 + 2 * k + h))
    ybank = (0, 7)

    g.sync.dma_start(T.w1t[:], T.w1[:]).then_inc(S.ld_w1, 16)
    g.scalar.dma_start(T.xt[:], T.x[:]).then_inc(S.ld_x, 16)
    g.sync.dma_start(T.et[:], T.res[:]).then_inc(S.ld_e, 16)
    g.sync.wait_ge(S.z1, 1)
    g.sync.dma_start(T.w2t[:], T.w2[:]).then_inc(S.ld_w2, 16)

    sent = 0
    g.wait_ge(S.q_w1, 1)
    for rnd in _w1_rounds(topo, cores, r):
        for buf, cast in ((T.w1q, True), (T.w1s, False)):
            view = buf[:, slot(r)].bitcast(u8) if cast else buf[:, slot(r)]
            trs = []
            for p, m in rnd:
                rid, pid = topo.addr(cores[p], core)
                trs.append(RemoteDMATransfer(dst_ids=[DstId(rid=rid, pnc=pid)], dma_engine_mask=m,
                                             remote_sem=S["aw%d" % r], src=view, dst=view))
                sent += _count(m)
            g.remote_dma_fused(trs, local_sem=S.sent)
    hdst = cores[(r - 1) % N]
    hmask = topo.mask(core, hdst)
    rid, pid = topo.addr(hdst, core)
    for h in range(2):
        g.wait_ge(S["q_h%d" % h], 1)
        g.remote_dma(out_ap=T.gq[:, half(h)].bitcast(u8), in_ap=T.hq[:, half(h)].bitcast(u8), remote_sem=S["ah%d" % h],
                     local_sem=S.sent, pid=pid, routing_id=rid, dma_engine_mask=hmask)
        g.remote_dma(out_ap=T.gs[:, half(h)], in_ap=T.hs[:, half(h)], remote_sem=S["ah%d" % h],
                     local_sem=S.sent, pid=pid, routing_id=rid, dma_engine_mask=hmask)
        sent += 2 * _count(hmask)
    g.wait_ge(S.sent, sent)

    te = g.tensor
    te.wait_ge(S.q_w1, 1)
    te.wait_ge(S.q_x, 1)
    seen = {r}
    for u, (j, c0, n, bank) in enumerate(units):
        if j not in seen:
            te.wait_ge(S["aw%d" % j], 2 * arrival(j)[2])
            seen.add(j)
        te.matmul_mx(T.ps[:, bank * 512:bank * 512 + n], T.w1q[:, slot(j)], T.w1s[:, slot(j)],
                     T.xq[:, c0:c0 + n], T.xs[:, c0:c0 + n], True, True).then_inc(S["z%d" % u], 1)
    te.wait_ge(S.q_h0, 1)
    te.wait_ge(S.q_h1, 1)
    te.wait_ge(S.q_w2, 1)
    for h in range(2):
        o = T.ps[:, ybank[h] * 512:ybank[h] * 512 + HALF]
        te.matmul_mx(o, T.w2q[:, slot(0)], T.w2s[:, slot(0)], T.hq[:, half(h)], T.hs[:, half(h)], True, False)
    hsrc = cores[(r + 1) % N]
    for h in range(2):
        te.wait_ge(S["ah%d" % h], 2 * _count(topo.mask(hsrc, core)))
        o = T.ps[:, ybank[h] * 512:ybank[h] * 512 + HALF]
        te.matmul_mx(o, T.w2q[:, slot(1)], T.w2s[:, slot(1)], T.gq[:, half(h)], T.gs[:, half(h)],
                     False, True).then_inc(S["y%d" % h], 1)

    sc = g.scalar
    for u, (j, c0, n, bank) in enumerate(units):
        b = (j - r) % N
        sc.wait_ge(S["z%d" % u], 1)
        sc.activation(T.at[:, b * NC + c0:b * NC + c0 + n], T.ps[:, bank * 512:bank * 512 + n],
                      ActivationFunctionType.Relu, scale=SCALE).then_inc(S["a%d" % u], 1)
    sc.wait_ge(S.y1, 1)
    sc.activation(T.yt[:, half(1)], T.ps[:, ybank[1] * 512:ybank[1] * 512 + HALF],
                  ActivationFunctionType.Copy).then_inc(S.c1, 1)

    ve = g.vector
    ve.wait_ge(S.ld_w1, 16)
    ve.quantize_mx(T.w1q[:, slot(r)], T.w1s[:, slot(r)], T.w1t[:]).then_inc(S.q_w1, 1)
    ve.wait_ge(S.ld_x, 16)
    ve.quantize_mx(T.xq[:], T.xs[:], T.xt[:]).then_inc(S.q_x, 1)
    ve.wait_ge(S.ld_e, 16)
    for u, (j, c0, n, bank) in enumerate(units):
        b = (j - r) % N
        ve.wait_ge(S["a%d" % u], 1)
        ve.tensor_tensor(T.ht[:, 4 * c0 + b:4 * (c0 + n):4], T.at[:, b * NC + c0:b * NC + c0 + n],
                         T.et[:, 4 * c0 + b:4 * (c0 + n):4], AluOpType.add).then_inc(S["d%d" % u], 1)
        if u in (N - 1, 2 * N - 2):
            h = 0 if u == N - 1 else 1
            for v in range(0 if h == 0 else N, u + 1):
                ve.wait_ge(S["d%d" % v], 1)
            ve.quantize_mx(T.hq[:, half(h)], T.hs[:, half(h)],
                           T.ht[:, 4 * h * HALF:4 * (h + 1) * HALF]).then_inc(S["q_h%d" % h], 1)
    ve.wait_ge(S.ld_w2, 16)
    ve.quantize_mx(T.w2q[:], T.w2s[:], T.w2t[:]).then_inc(S.q_w2, 1)
    ve.wait_ge(S.y0, 1)
    ve.tensor_copy(T.yt[:, half(0)], T.ps[:, ybank[0] * 512:ybank[0] * 512 + HALF]).then_inc(S.c0, 1)

    for h in range(2):
        g.sync.wait_ge(S["c%d" % h], 1)
        g.sync.dma_start(T.y[:, half(h)], T.yt[:, half(h)]).then_inc(S.st, 16)
    g.sync.wait_ge(S.st, 32)
